import numpy as np
import ml_dtypes


def mxq(x, axis, fmt="e4m3"):
    dtype, down = {"e4m3": (ml_dtypes.float8_e4m3fn, 7), "e5m2": (ml_dtypes.float8_e5m2, 14)}[fmt]
    v = np.moveaxis(np.asarray(x, np.float32).astype(ml_dtypes.bfloat16).astype(np.float64), axis, -1)
    blocks = v.reshape(v.shape[:-1] + (-1, 32))
    amax = np.abs(blocks).max(-1, keepdims=True)
    byte = np.maximum(np.where(amax > 0, np.frexp(amax)[1] - 1 + 127, 0) - down, 1)
    scale = np.exp2(byte - 127.0)
    codes = (blocks / scale).astype(np.float32).astype(dtype).astype(np.float64)
    return np.moveaxis((codes * scale).reshape(v.shape), -1, axis)


WIDE = False


def mx_kscale(k):
    if not WIDE:
        return np.ones(k)
    levels = np.array([30, -30])
    if k % 512:
        return np.exp2(np.random.permutation(np.resize(levels, k // 32))).repeat(32)
    a = np.empty((k // 512, 16))
    for p in range(k // 512):
        a[p, :8] = np.random.permutation(np.resize(levels, 8))
        for g in range(8):
            far = levels[np.abs(levels - a[p, g]) >= 10]
            a[p, g + 8] = far[np.random.randint(len(far))]
    return np.exp2(a.ravel()).repeat(32)


def f64(x):
    return np.asarray(x).astype(np.float64)


def striped(idx):
    return np.tile(idx.reshape(-1, 16).T, (8, 1)).astype(np.uint16)


def unstriped(offs):
    return offs[:16].T.reshape(-1).astype(np.int64)


E2M1 = np.array([0.0, 0.5, 1.0, 1.5, 2.0, 3.0, 4.0, 6.0, -0.0, -0.5, -1.0, -1.5, -2.0, -3.0, -4.0, -6.0])


def pack_weight(w, fmt):
    k, n = w.shape
    w = f64(np.asarray(w, np.float32).astype(ml_dtypes.bfloat16)).reshape(k // 32, 32, n)
    amax = np.abs(w).max(1)
    if fmt == "e4m3":
        byte = np.frexp(amax)[1] - 1 + 127 - 7
    else:
        mant, ex = np.frexp(amax / 6.0)
        byte = np.where(mant > 0.5, ex, ex - 1) + 127
    byte = np.clip(np.where(amax > 0, byte, 1), 1, 254)
    scaled = (w * np.exp2(127.0 - byte)[:, None, :]).reshape(k, n).astype(np.float32)
    by_word = np.ascontiguousarray(scaled.reshape(k // 512, 128, 4, n).transpose(0, 1, 3, 2))
    if fmt == "e4m3":
        words = by_word.astype(ml_dtypes.float8_e4m3fn).view(np.uint8)
    else:
        c = by_word.astype(ml_dtypes.float4_e2m1fn).view(np.uint8) & 0xF
        words = (c[..., 0::2] | (c[..., 1::2] << 4)).reshape(k // 512, 128, 2 * n)
    return np.ascontiguousarray(words), np.ascontiguousarray(byte.astype(np.uint8).reshape(k // 512, 16, n))


def unpack_weight(words, scales, fmt):
    g, _, n = scales.shape
    words = np.ascontiguousarray(words).reshape(g, 128, n, -1)
    if fmt == "e4m3":
        vals = words.view(ml_dtypes.float8_e4m3fn).astype(np.float64)
    else:
        nib = np.empty((g, 128, n, 4), np.uint8)
        nib[..., 0::2] = words & 0xF
        nib[..., 1::2] = words >> 4
        vals = E2M1[nib]
    vals = vals * np.repeat(np.exp2(scales.astype(np.float64) - 127.0), 8, axis=1)[..., None]
    return vals.transpose(0, 1, 3, 2).reshape(g * 512, n)


def relu(v):
    return np.maximum(v, 0.0)


def d_relu(v):
    return (v > 0).astype(np.float64)


K, T, E, C, H, N = 384, 1024, 4, 512, 512, 1024


def by_expert(wq, xq):
    return np.concatenate([wq[e].T @ xq[:, e * C:(e + 1) * C] for e in range(E)], axis=1)


def setup_inputs():
    n = np.random.standard_normal
    s = mx_kscale(N)[:, None]
    u = mx_kscale(H)
    first = np.random.permutation(np.repeat(np.arange(E), T // E))
    second = (first + 1 + np.random.permutation(np.repeat(np.arange(E - 1), -(-T // (E - 1)))[:T])) % E
    while np.bincount(second, minlength=E).max() != T // E:
        load = np.bincount(second, minlength=E); hi, lo = int(load.argmax()), int(load.argmin())
        t = np.flatnonzero((second == hi) & (first != lo))[0]; second[t] = lo
    slot_token = np.empty(E * C, np.int64); pos = np.empty((2, T), np.int64); fill = np.zeros(E, np.int64)
    place = np.stack([np.random.permutation(C) for _ in range(E)])
    for r, deal in enumerate((first, second)):
        for t in np.random.permutation(T):
            e = deal[t]; j = e * C + place[e, fill[e]]; fill[e] += 1; slot_token[j] = t; pos[r, t] = j
    g = np.random.uniform(0.2, 0.8, T)
    w_slot = np.empty(E * C); w_slot[pos[0]] = g; w_slot[pos[1]] = 1.0 - g
    w2 = [pack_weight(m, "e2m1") for m in n((E, N, H)) / np.sqrt(N) / s[None] * u[None, None, :]]
    w1 = [pack_weight(m, "e2m1") for m in n((E, H, K)) / np.sqrt(H) / u[None, :, None]]
    w3 = [pack_weight(m, "e2m1") for m in n((E, H, K)) / np.sqrt(H) / u[None, :, None]]
    return {
        "dyT": (n((N, T)) * s).astype(np.float32),
        "a1": n((H, E * C)).astype(np.float32),
        "a3": n((H, E * C)).astype(np.float32),
        "w2_words": np.stack([m[0] for m in w2]),
        "w2_scales": np.stack([m[1] for m in w2]),
        "w1_words": np.stack([m[0] for m in w1]),
        "w1_scales": np.stack([m[1] for m in w1]),
        "w3_words": np.stack([m[0] for m in w3]),
        "w3_scales": np.stack([m[1] for m in w3]),
        "gate": np.tile(w_slot, (N, 1)).astype(np.float32),
        "offs": striped(slot_token),
        "pos1": striped(pos[0]),
        "pos2": striped(pos[1]),
    }


def reference(dyT, a1, a3, w2_words, w2_scales, w1_words, w1_scales, w3_words, w3_scales, gate, offs, pos1, pos2):
    idx = unstriped(offs)
    w2 = np.stack([unpack_weight(w2_words[e], w2_scales[e], "e2m1") for e in range(E)])
    w1 = np.stack([unpack_weight(w1_words[e], w1_scales[e], "e2m1") for e in range(E)])
    w3 = np.stack([unpack_weight(w3_words[e], w3_scales[e], "e2m1") for e in range(E)])
    gq = mxq(f64(gate) * f64(dyT)[:, idx], 0, "e5m2")
    dh = by_expert(w2, gq)
    da1 = dh * f64(a3) * d_relu(f64(a1))
    da3 = dh * relu(f64(a1))
    dx = by_expert(w1, mxq(da1, 0, "e5m2")) + by_expert(w3, mxq(da3, 0, "e5m2"))
    return dx[:, unstriped(pos1)] + dx[:, unstriped(pos2)]

@@ -1,0 +1,261 @@
+from contextlib import ExitStack
+
+import concourse.mybir as mybir
+
+K, T, E, C, H, N = 384, 1024, 4, 512, 512, 1024
+S = E * C
+P = 128
+PACK = 4
+PASSES = N // (P * PACK)
+KB = K // P
+
+FLOPS = 2 * S * (N * H + 2 * H * K)
+BYTES = 4 * (N * T + 2 * H * S + S + K * T) + E * (N * H + 2 * H * K) // 2 + E * (N * H + 2 * H * K) // 32 + 2 * (S + 2 * T)
+
+F32 = mybir.dt.float32
+BF16 = mybir.dt.bfloat16
+I32 = mybir.dt.int32
+U32 = mybir.dt.uint32
+U16 = mybir.dt.uint16
+U8 = mybir.dt.uint8
+E5X4 = mybir.dt.float8_e5m2_x4
+E2X4 = mybir.dt.float4_e2m1fn_x4
+MULT = mybir.AluOpType.mult
+ADD = mybir.AluOpType.add
+RELU = mybir.ActivationFunctionType.Relu
+SIGN = mybir.ActivationFunctionType.Sign
+
+
+def tile_moe_bdx_glu_relu_kernel(tc, dyT, a1, a3, w2_words, w2_scales, w1_words, w1_scales, w3_words, w3_scales, gate, offs, pos1, pos2, out):
+    nc = tc.nc
+    with ExitStack() as ctx:
+        keep = ctx.enter_context(tc.tile_pool(name="keep", bufs=1))
+        wins = ctx.enter_context(tc.tile_pool(name="wins", bufs=8))
+        two = ctx.enter_context(tc.tile_pool(name="two", bufs=2))
+        three = ctx.enter_context(tc.tile_pool(name="three", bufs=3))
+        four = ctx.enter_context(tc.tile_pool(name="four", bufs=4))
+        pdh = ctx.enter_context(tc.psum_pool(name="pdh", bufs=5))
+        pdx = ctx.enter_context(tc.psum_pool(name="pdx", bufs=3))
+
+        lo = keep.tile([P, S // 16], U16, name="lo")
+        lp1 = keep.tile([P, T // 16], U16, name="lp1")
+        lp2 = keep.tile([P, T // 16], U16, name="lp2")
+        gt = keep.tile([P, S], F32, name="gt")
+        w2p = keep.tile([P, E * PASSES * 2 * H], U8, name="w2p", align_bytes=64)
+        w2r = keep.tile([P, PASSES * H], U8, name="w2r", align_bytes=64)
+        w2s = keep.tile([P, E * PASSES * H], U8, name="w2s", align_bytes=64)
+        wk = [keep.tile([P, E * 2 * K], U8, name=f"wk{x}", align_bytes=64) for x in range(2)]
+        wks = [keep.tile([P, E * K], U8, name=f"wks{x}", align_bytes=64) for x in range(2)]
+        dx = [keep.tile([P, S], F32, name=f"dx{b}") for b in range(KB)]
+        for t in [w2r, w2s] + wks:
+            nc.gpsimd.memset(t[:].bitcast(I32), 0)
+
+        dy_v = dyT.rearrange("(s p t) c -> s t p c", s=PASSES, t=PACK)
+        win = {}
+
+        def load_win(s, t):
+            win[s, t] = wins.tile([P, T], F32, name="win")
+            nc.sync.dma_start(win[s, t][:], dy_v[s, t])
+
+        def load_gate(e):
+            nc.sync.dma_start(gt[:, e * C:(e + 1) * C], gate[0:P, e * C:(e + 1) * C])
+
+        def load_scales(tile, dram, n):
+            v = dram.bitcast(I32).rearrange("e s (q r) i -> r q (e s) i", r=4)
+            for r in range(4):
+                nc.sync.dma_start(tile[r:P:32, :].bitcast(I32).rearrange("q (g i) -> q g i", i=n // 4), v[r])
+
+        def load_w2_scales(e):
+            v = w2_scales[e].bitcast(I32).rearrange("s (q r) i -> r q s i", r=4)
+            for r in range(4):
+                nc.sync.dma_start(w2r[4 * e + r:P:32, :].bitcast(I32).rearrange("q (s i) -> q s i", s=PASSES), v[r])
+
+        def spread_w2_scales():
+            n = PASSES * H
+            w2q = keep.tile([P, n], U8, name="w2q", align_bytes=64)
+            nc.vector.tensor_copy(
+                out=w2q[:].rearrange("p (s t m) -> p s t m", s=PASSES, t=PACK),
+                in_=w2r[:].rearrange("p (s m t) -> p s t m", s=PASSES, t=PACK))
+            for e in range(E):
+                for r in range(4):
+                    nc.sync.dma_start(w2s[r:P:32, e * n:(e + 1) * n].bitcast(I32), w2q[4 * e + r:P:32, :].bitcast(I32))
+
+        w2raw = {}
+
+        def load_w2(e):
+            w2raw[e] = two.tile([P, PASSES * 2 * H], U8, name="w2raw")
+            nc.sync.dma_start(w2raw[e][:].bitcast(I32).rearrange("p (s b) -> p s b", s=PASSES), w2_words[e].bitcast(I32).rearrange("s p b -> p s b"))
+
+        def load_wk(x, dram):
+            nc.sync.dma_start(wk[x][:].bitcast(I32).rearrange("p (e b) -> p e b", e=E), dram.bitcast(I32).rearrange("e s p b -> p (e s) b"))
+
+        am = {}
+        a_v = [a.rearrange("(p t) (e c) -> e p t c", t=PACK, e=E) for a in (a3, a1)]
+
+        def load_a(e):
+            am[e] = three.tile([P, 2, PACK, C], F32, name="am")
+            for x in (1, 0):
+                nc.sync.dma_start(am[e][:, x], a_v[x][e])
+
+        nc.sync.dma_start(lo[:], offs)
+        load_win(0, 0)
+        load_gate(0)
+        load_win(0, 1)
+        load_win(0, 2)
+        load_win(0, 3)
+        load_gate(1)
+        load_w2(0)
+        for t in range(PACK):
+            load_win(1, t)
+        load_w2(1)
+        for e in range(E):
+            load_w2_scales(e)
+        load_a(0)
+        load_gate(2)
+        load_gate(3)
+        load_w2(2)
+        load_wk(0, w1_words)
+        load_wk(1, w3_words)
+        load_scales(wks[0], w1_scales, K)
+        load_scales(wks[1], w3_scales, K)
+        load_w2(3)
+        load_a(1)
+        load_a(2)
+        load_a(3)
+        nc.sync.dma_start(lp1[:], pos1)
+        nc.sync.dma_start(lp2[:], pos2)
+
+        def permute(e):
+            n = PASSES * 2 * H
+            nc.vector.tensor_copy(
+                out=w2p[:, e * n:(e + 1) * n].bitcast(U16).rearrange("p (s t m) -> p s t m", s=PASSES, t=PACK),
+                in_=w2raw[e][:].bitcast(U16).rearrange("p (s m t) -> p s t m", s=PASSES, t=PACK))
+
+        gi, gq, gs = {}, {}, {}
+
+        def gathers(e, s):
+            g4 = three.tile([P, PACK, C], F32, name="g4")
+            for t in range(PACK):
+                nc.vector.tensor_tensor(g4[:, t, :], win[s, t][:].indirect(lo[:, e * C // 16:(e + 1) * C // 16]), gt[:, e * C:(e + 1) * C], MULT)
+            gi[e, s] = two.tile([P, C * PACK], BF16, name="gi", align_bytes=64)
+            nc.scalar.copy(out=gi[e, s][:].rearrange("p (n t) -> p n t", t=PACK), in_=g4[:].rearrange("p t n -> p n t"))
+
+        def quant_g(e, s):
+            gq[e, s] = four.tile([P, C], U32, name="gq", align_bytes=64)
+            gs[e, s] = four.tile([P, C], U8, name="gs", align_bytes=64)
+            nc.vector.quantize_mx(out=gq[e, s][:].bitcast(E5X4), scales=gs[e, s][:], in_=gi[e, s][:])
+
+        dh = {}
+
+        def mm_dh(e):
+            for t in range(PACK):
+                dh[e, t] = pdh.tile([P, C], F32, name="dh")
+                for s in range(PASSES):
+                    b = ((e * PASSES + s) * PACK + t) * P
+                    nc.tensor.matmul_mx(
+                        out=dh[e, t][:], lhsT=w2p[:, 2 * b:2 * (b + P)].bitcast(E2X4), lhsT_scale=w2s[:, b:b + P],
+                        rhs=gq[e, s][:].bitcast(E5X4), rhs_scale=gs[e, s][:], start=(s == 0), stop=(s == PASSES - 1))
+
+        mk = {}
+
+        def masks(e):
+            mk[e] = two.tile([P, C * PACK], BF16, name="mk")
+            nc.scalar.activation(am[e][:, 1], am[e][:, 1], RELU)
+            nc.scalar.activation(mk[e][:].rearrange("p (n t) -> p n t", t=PACK), am[e][:, 1].rearrange("p t n -> p n t"), SIGN)
+
+        z, zi = {}, {}
+
+        def products(e, split=False):
+            z[e] = two.tile([P, 2, PACK, C], BF16, name="z")
+            if split:
+                for x in (1, 0):
+                    for t in range(PACK):
+                        nc.vector.tensor_tensor(z[e][:, x, t, :], dh[e, t][:], am[e][:, x, t, :], MULT)
+                return
+            for t in range(PACK):
+                nc.vector.tensor_tensor(z[e][:, :, t, :], dh[e, t][:].unsqueeze(1).to_broadcast([P, 2, C]), am[e][:, :, t, :], MULT)
+
+        def interleave(e, vector=()):
+            zi[e] = [two.tile([P, C * PACK], BF16, name=f"zi{x}", align_bytes=64) for x in range(2)]
+            for x in (1, 0):
+                o = zi[e][x][:].rearrange("p (n t) -> p n t", t=PACK)
+                i = z[e][:, x].rearrange("p t n -> p n t")
+                if x in vector:
+                    nc.vector.tensor_copy(out=o, in_=i)
+                else:
+                    nc.scalar.copy(out=o, in_=i)
+
+        dq, ds = {}, {}
+
+        def quant_d(e):
+            for x in (1, 0):
+                if x == 0:
+                    nc.vector.tensor_tensor(zi[e][0][:], zi[e][0][:], mk[e][:], MULT)
+                dq[e, x] = two.tile([P, C], U32, name=f"dq{x}", align_bytes=64)
+                ds[e, x] = two.tile([P, C], U8, name=f"ds{x}", align_bytes=64)
+                nc.vector.quantize_mx(out=dq[e, x][:].bitcast(E5X4), scales=ds[e, x][:], in_=zi[e][x][:])
+
+        def mm_dx(e):
+            for b in range(KB):
+                acc = pdx.tile([P, C], F32, name="acc")
+                for x in (1, 0):
+                    c = e * K + b * P
+                    nc.tensor.matmul_mx(
+                        out=acc[:], lhsT=wk[x][:, 2 * c:2 * (c + P)].bitcast(E2X4), lhsT_scale=wks[x][:, c:c + P],
+                        rhs=dq[e, x][:].bitcast(E5X4), rhs_scale=ds[e, x][:], start=(x == 1), stop=(x == 0))
+                nc.scalar.copy(out=dx[b][:, e * C:(e + 1) * C], in_=acc[:])
+
+        gathers(0, 0)
+        permute(0)
+        gathers(1, 0)
+        quant_g(0, 0)
+        permute(1)
+        gathers(0, 1)
+        quant_g(1, 0)
+        gathers(1, 1)
+        quant_g(0, 1)
+        spread_w2_scales()
+        mm_dh(0)
+        masks(0)
+        permute(2)
+        gathers(2, 0)
+        quant_g(1, 1)
+        products(0)
+        interleave(0)
+        mm_dh(1)
+        permute(3)
+        gathers(2, 1)
+        quant_g(2, 0)
+        quant_d(0)
+        mm_dx(0)
+        masks(1)
+        gathers(3, 0)
+        quant_g(2, 1)
+        products(1)
+        interleave(1)
+        mm_dh(2)
+        gathers(3, 1)
+        quant_g(3, 0)
+        quant_d(1)
+        mm_dx(1)
+        masks(2)
+        products(2)
+        quant_g(3, 1)
+        interleave(2)
+        mm_dh(3)
+        masks(3)
+        products(3, split=True)
+        interleave(3)
+        quant_d(2)
+        mm_dx(2)
+        quant_d(3)
+        mm_dx(3)
+
+        for b in range(KB):
+            y = [wins.tile([P, T], F32, name="win") for r in range(2)]
+            parts = [(nc.gpsimd, 0, T)] if b < KB - 1 else [(nc.gpsimd, 0, T // 2), (nc.vector, T // 2, T)]
+            for eng, c0, c1 in parts:
+                for r, lp in enumerate((lp1, lp2)):
+                    nc.vector.tensor_copy(y[r][:, c0:c1], dx[b][:].indirect(lp[:, c0 // 16:c1 // 16]))
+                eng.tensor_tensor(y[0][:, c0:c1], y[0][:, c0:c1], y[1][:, c0:c1], ADD)
+                nc.sync.dma_start(out[b * P:(b + 1) * P, c0:c1], y[0][:, c0:c1])

@@ -138,59 +138,51 @@ def tile_moe_bdx_glu_relu_kernel(tc, dyT, a1, a3, w2_words, w2_scales, w1_words,
             for t in range(PACK):
                 nc.vector.tensor_tensor(g4[:, t, :], win[s, t][:].indirect(lo[:, e * C // 16:(e + 1) * C // 16]), gt[:, e * C:(e + 1) * C], MULT)
             gi[e, s] = two.tile([P, C * PACK], BF16, name="gi", align_bytes=64)
-            nc.scalar.copy(out=gi[e, s][:].rearrange("p (n t) -> p n t", t=PACK), in_=g4[:].rearrange("p t n -> p n t"))
+            nc.scalar.copy(out=gi[e, s][:].rearrange("p (c i t) -> p c t i", i=4, t=PACK), in_=g4[:].rearrange("p t (c i) -> p c t i", i=4))
 
         def quant_g(e, s):
             gq[e, s] = four.tile([P, C], U32, name="gq", align_bytes=64)
             gs[e, s] = four.tile([P, C], U8, name="gs", align_bytes=64)
             nc.vector.quantize_mx(out=gq[e, s][:].bitcast(E5X4), scales=gs[e, s][:], in_=gi[e, s][:])
 
-        dh = {}
+        hs = {}
 
         def mm_dh(e):
+            hs[e] = two.tile([P, PACK, C], F32, name="hs")
             for t in range(PACK):
-                dh[e, t] = pdh.tile([P, C], F32, name="dh")
+                dh = pdh.tile([P, C], F32, name="dh")
                 for s in range(PASSES):
                     b = ((e * PASSES + s) * PACK + t) * P
                     nc.tensor.matmul_mx(
-                        out=dh[e, t][:], lhsT=w2p[:, 2 * b:2 * (b + P)].bitcast(E2X4), lhsT_scale=w2s[:, b:b + P],
+                        out=dh[:], lhsT=w2p[:, 2 * b:2 * (b + P)].bitcast(E2X4), lhsT_scale=w2s[:, b:b + P],
                         rhs=gq[e, s][:].bitcast(E5X4), rhs_scale=gs[e, s][:], start=(s == 0), stop=(s == PASSES - 1))
+                nc.scalar.copy(out=hs[e][:, t, :], in_=dh[:])
 
         mk = {}
 
         def masks(e):
             mk[e] = two.tile([P, C * PACK], BF16, name="mk")
             nc.scalar.activation(am[e][:, 1], am[e][:, 1], RELU)
-            nc.scalar.activation(mk[e][:].rearrange("p (n t) -> p n t", t=PACK), am[e][:, 1].rearrange("p t n -> p n t"), SIGN)
+            nc.scalar.activation(mk[e][:].rearrange("p (c i t) -> p c t i", i=4, t=PACK), am[e][:, 1].rearrange("p t (c i) -> p c t i", i=4), SIGN)
 
-        z, zi = {}, {}
+        zi = {}
 
-        def products(e, split=False):
-            z[e] = two.tile([P, 2, PACK, C], BF16, name="z")
-            if split:
-                for x in (1, 0):
-                    for t in range(PACK):
-                        nc.vector.tensor_tensor(z[e][:, x, t, :], dh[e, t][:], am[e][:, x, t, :], MULT)
-                return
-            for t in range(PACK):
-                nc.vector.tensor_tensor(z[e][:, :, t, :], dh[e, t][:].unsqueeze(1).to_broadcast([P, 2, C]), am[e][:, :, t, :], MULT)
+        def quads(ap):
+            return ap.rearrange("p t (c i) -> p c t i", i=4)
 
-        def interleave(e, vector=()):
+        def woven(ap):
+            return ap.rearrange("p (c i t) -> p c t i", i=4, t=PACK)
+
+        def products(e):
             zi[e] = [two.tile([P, C * PACK], BF16, name=f"zi{x}", align_bytes=64) for x in range(2)]
-            for x in (1, 0):
-                o = zi[e][x][:].rearrange("p (n t) -> p n t", t=PACK)
-                i = z[e][:, x].rearrange("p t n -> p n t")
-                if x in vector:
-                    nc.vector.tensor_copy(out=o, in_=i)
-                else:
-                    nc.scalar.copy(out=o, in_=i)
+            for x in (0, 1):
+                nc.vector.tensor_tensor(woven(zi[e][x][:]), quads(hs[e][:]), quads(am[e][:, x]), MULT)
 
         dq, ds = {}, {}
 
         def quant_d(e):
+            nc.vector.tensor_tensor(zi[e][0][:], zi[e][0][:], mk[e][:], MULT)
             for x in (1, 0):
-                if x == 0:
-                    nc.vector.tensor_tensor(zi[e][0][:], zi[e][0][:], mk[e][:], MULT)
                 dq[e, x] = two.tile([P, C], U32, name=f"dq{x}", align_bytes=64)
                 ds[e, x] = two.tile([P, C], U8, name=f"ds{x}", align_bytes=64)
                 nc.vector.quantize_mx(out=dq[e, x][:].bitcast(E5X4), scales=ds[e, x][:], in_=zi[e][x][:])
@@ -220,34 +212,30 @@ def tile_moe_bdx_glu_relu_kernel(tc, dyT, a1, a3, w2_words, w2_scales, w1_words,
         permute(2)
         gathers(2, 0)
         quant_g(1, 1)
-        products(0)
-        interleave(0)
         mm_dh(1)
+        products(0)
         permute(3)
         gathers(2, 1)
-        quant_g(2, 0)
         quant_d(0)
+        quant_g(2, 0)
         mm_dx(0)
         masks(1)
-        gathers(3, 0)
-        quant_g(2, 1)
         products(1)
-        interleave(1)
-        mm_dh(2)
-        gathers(3, 1)
-        quant_g(3, 0)
+        gathers(3, 0)
         quant_d(1)
+        quant_g(2, 1)
+        mm_dh(2)
         mm_dx(1)
         masks(2)
+        gathers(3, 1)
+        quant_g(3, 0)
         products(2)
         quant_g(3, 1)
-        interleave(2)
         mm_dh(3)
         masks(3)
-        products(3, split=True)
-        interleave(3)
         quant_d(2)
         mm_dx(2)
+        products(3)
         quant_d(3)
         mm_dx(3)
 

@@ -10,6 +10,7 @@ PASSES = N // (P * PACK)
 KB = K // P
 
 FLOPS = 2 * S * (N * H + 2 * H * K)
+W = T + 16
 BYTES = 4 * (N * T + 2 * H * S + S + K * T) + E * (N * H + 2 * H * K) // 2 + E * (N * H + 2 * H * K) // 32 + 2 * (S + 2 * T)
 
 F32 = mybir.dt.float32
@@ -32,7 +33,6 @@ def tile_moe_bdx_glu_relu_kernel(tc, dyT, a1, a3, w2_words, w2_scales, w1_words,
         keep = ctx.enter_context(tc.tile_pool(name="keep", bufs=1))
         wins = ctx.enter_context(tc.tile_pool(name="wins", bufs=8))
         two = ctx.enter_context(tc.tile_pool(name="two", bufs=2))
-        three = ctx.enter_context(tc.tile_pool(name="three", bufs=3))
         four = ctx.enter_context(tc.tile_pool(name="four", bufs=4))
         pdh = ctx.enter_context(tc.psum_pool(name="pdh", bufs=5))
         pdx = ctx.enter_context(tc.psum_pool(name="pdx", bufs=3))
@@ -54,8 +54,9 @@ def tile_moe_bdx_glu_relu_kernel(tc, dyT, a1, a3, w2_words, w2_scales, w1_words,
         win = {}
 
         def load_win(s, t):
-            win[s, t] = wins.tile([P, T], F32, name="win")
-            nc.sync.dma_start(win[s, t][:], dy_v[s, t])
+            win[s, t] = wins.tile([P, W], F32, name="win")
+            nc.gpsimd.memset(win[s, t][:, T:], 0.0)
+            nc.sync.dma_start(win[s, t][:, 0:T], dy_v[s, t])
 
         def load_gate(e):
             nc.sync.dma_start(gt[:, e * C:(e + 1) * C], gate[0:P, e * C:(e + 1) * C])
@@ -65,20 +66,17 @@ def tile_moe_bdx_glu_relu_kernel(tc, dyT, a1, a3, w2_words, w2_scales, w1_words,
             for r in range(4):
                 nc.sync.dma_start(tile[r:P:32, :].bitcast(I32).rearrange("q (g i) -> q g i", i=n // 4), v[r])
 
-        def load_w2_scales(e):
-            v = w2_scales[e].bitcast(I32).rearrange("s (q r) i -> r q s i", r=4)
-            for r in range(4):
-                nc.sync.dma_start(w2r[4 * e + r:P:32, :].bitcast(I32).rearrange("q (s i) -> q s i", s=PASSES), v[r])
+        def load_w2_scales():
+            for e in range(E):
+                nc.sync.dma_start(w2r[32 * e:32 * e + 16, :].bitcast(I32).rearrange("f (s i) -> f s i", s=PASSES), w2_scales[e].bitcast(I32).rearrange("s f i -> f s i"))
 
         def spread_w2_scales():
             n = PASSES * H
             w2q = keep.tile([P, n], U8, name="w2q", align_bytes=64)
-            nc.vector.tensor_copy(
-                out=w2q[:].rearrange("p (s t m) -> p s t m", s=PASSES, t=PACK),
-                in_=w2r[:].rearrange("p (s m t) -> p s t m", s=PASSES, t=PACK))
+            nc.vector.tensor_copy(out=w2q[:].rearrange("p (s t m) -> p s t m", s=PASSES, t=PACK), in_=w2r[:].rearrange("p (s m t) -> p s t m", s=PASSES, t=PACK))
             for e in range(E):
                 for r in range(4):
-                    nc.sync.dma_start(w2s[r:P:32, e * n:(e + 1) * n].bitcast(I32), w2q[4 * e + r:P:32, :].bitcast(I32))
+                    nc.sync.dma_start(w2s[r:P:32, e * n:(e + 1) * n].bitcast(I32), w2q[32 * e + r:32 * e + 16:4, :].bitcast(I32))
 
         w2raw = {}
 
@@ -93,7 +91,7 @@ def tile_moe_bdx_glu_relu_kernel(tc, dyT, a1, a3, w2_words, w2_scales, w1_words,
         a_v = [a.rearrange("(p t) (e c) -> e p t c", t=PACK, e=E) for a in (a3, a1)]
 
         def load_a(e):
-            am[e] = three.tile([P, 2, PACK, C], F32, name="am")
+            am[e] = two.tile([P, 2, PACK, C], F32, name="am")
             for x in (1, 0):
                 nc.sync.dma_start(am[e][:, x], a_v[x][e])
 
@@ -101,15 +99,14 @@ def tile_moe_bdx_glu_relu_kernel(tc, dyT, a1, a3, w2_words, w2_scales, w1_words,
         load_win(0, 0)
         load_gate(0)
         load_win(0, 1)
+        load_gate(1)
         load_win(0, 2)
         load_win(0, 3)
-        load_gate(1)
         load_w2(0)
         for t in range(PACK):
             load_win(1, t)
         load_w2(1)
-        for e in range(E):
-            load_w2_scales(e)
+        load_w2_scales()
         load_a(0)
         load_gate(2)
         load_gate(3)
@@ -133,12 +130,17 @@ def tile_moe_bdx_glu_relu_kernel(tc, dyT, a1, a3, w2_words, w2_scales, w1_words,
 
         gi, gq, gs = {}, {}, {}
 
-        def gathers(e, s):
-            g4 = three.tile([P, PACK, C], F32, name="g4")
+        def gathers(e0, s, cuts=(1024,)):
+            g4 = two.tile([P, PACK, 2 * C], F32, name="g4")
             for t in range(PACK):
-                nc.vector.tensor_tensor(g4[:, t, :], win[s, t][:].indirect(lo[:, e * C // 16:(e + 1) * C // 16]), gt[:, e * C:(e + 1) * C], MULT)
-            gi[e, s] = two.tile([P, C * PACK], BF16, name="gi", align_bytes=64)
-            nc.scalar.copy(out=gi[e, s][:].rearrange("p (c i t) -> p c t i", i=4, t=PACK), in_=g4[:].rearrange("p t (c i) -> p c t i", i=4))
+                j = 0
+                for n in (cuts if t == 0 else (1024,)):
+                    j0 = e0 * C + j
+                    nc.vector.tensor_tensor(g4[:, t, j:j + n], win[s, t][:].indirect(lo[:, j0 // 16:(j0 + n) // 16]), gt[:, j0:j0 + n], MULT)
+                    j += n
+            for e in (e0, e0 + 1):
+                gi[e, s] = two.tile([P, C * PACK], BF16, name="gi", align_bytes=64)
+                nc.scalar.copy(out=gi[e, s][:].rearrange("p (c i t) -> p c t i", i=4, t=PACK), in_=g4[:, :, (e - e0) * C:(e - e0 + 1) * C].rearrange("p t (c i) -> p c t i", i=4))
 
         def quant_g(e, s):
             gq[e, s] = four.tile([P, C], U32, name="gq", align_bytes=64)
@@ -173,19 +175,23 @@ def tile_moe_bdx_glu_relu_kernel(tc, dyT, a1, a3, w2_words, w2_scales, w1_words,
         def woven(ap):
             return ap.rearrange("p (c i t) -> p c t i", i=4, t=PACK)
 
-        def products(e):
-            zi[e] = [two.tile([P, C * PACK], BF16, name=f"zi{x}", align_bytes=64) for x in range(2)]
-            for x in (0, 1):
-                nc.vector.tensor_tensor(woven(zi[e][x][:]), quads(hs[e][:]), quads(am[e][:, x]), MULT)
+        def product(e, x, parts=1):
+            if e not in zi:
+                zi[e] = two.tile([P, 2, C * PACK], BF16, name="zi", align_bytes=64)
+            w = P // parts
+            for c in range(0, P, w):
+                nc.vector.tensor_tensor(woven(zi[e][:, x])[:, c:c + w], quads(hs[e][:])[:, c:c + w], quads(am[e][:, x])[:, c:c + w], MULT)
 
         dq, ds = {}, {}
 
+        def mask_d(e):
+            nc.vector.tensor_tensor(zi[e][:, 0], zi[e][:, 0], mk[e][:], MULT)
+
         def quant_d(e):
-            nc.vector.tensor_tensor(zi[e][0][:], zi[e][0][:], mk[e][:], MULT)
             for x in (1, 0):
                 dq[e, x] = two.tile([P, C], U32, name=f"dq{x}", align_bytes=64)
                 ds[e, x] = two.tile([P, C], U8, name=f"ds{x}", align_bytes=64)
-                nc.vector.quantize_mx(out=dq[e, x][:].bitcast(E5X4), scales=ds[e, x][:], in_=zi[e][x][:])
+                nc.vector.quantize_mx(out=dq[e, x][:].bitcast(E5X4), scales=ds[e, x][:], in_=zi[e][:, x])
 
         def mm_dx(e):
             for b in range(KB):
@@ -197,51 +203,55 @@ def tile_moe_bdx_glu_relu_kernel(tc, dyT, a1, a3, w2_words, w2_scales, w1_words,
                         rhs=dq[e, x][:].bitcast(E5X4), rhs_scale=ds[e, x][:], start=(x == 1), stop=(x == 0))
                 nc.scalar.copy(out=dx[b][:, e * C:(e + 1) * C], in_=acc[:])
 
-        gathers(0, 0)
+        gathers(0, 0, (512, 512))
         permute(0)
-        gathers(1, 0)
         quant_g(0, 0)
         permute(1)
         gathers(0, 1)
         quant_g(1, 0)
-        gathers(1, 1)
-        quant_g(0, 1)
         spread_w2_scales()
+        quant_g(0, 1)
         mm_dh(0)
-        masks(0)
+        quant_g(1, 1)
         permute(2)
         gathers(2, 0)
-        quant_g(1, 1)
+        masks(0)
         mm_dh(1)
-        products(0)
+        product(0, 0)
+        product(0, 1)
+        mask_d(0)
         permute(3)
-        gathers(2, 1)
         quant_d(0)
         quant_g(2, 0)
+        quant_g(3, 0)
+        gathers(2, 1)
         mm_dx(0)
         masks(1)
-        products(1)
-        gathers(3, 0)
-        quant_d(1)
+        product(1, 0)
         quant_g(2, 1)
         mm_dh(2)
-        mm_dx(1)
-        masks(2)
-        gathers(3, 1)
-        quant_g(3, 0)
-        products(2)
+        product(1, 1, 2)
         quant_g(3, 1)
         mm_dh(3)
+        mask_d(1)
+        quant_d(1)
+        mm_dx(1)
+        masks(2)
+        product(2, 0)
+        product(2, 1)
         masks(3)
+        mask_d(2)
         quant_d(2)
         mm_dx(2)
-        products(3)
+        product(3, 0)
+        product(3, 1)
+        mask_d(3)
         quant_d(3)
         mm_dx(3)
 
         for b in range(KB):
-            y = [wins.tile([P, T], F32, name="win") for r in range(2)]
-            parts = [(nc.gpsimd, 0, T)] if b < KB - 1 else [(nc.gpsimd, 0, T // 2), (nc.vector, T // 2, T)]
+            y = [wins.tile([P, W], F32, name="win") for r in range(2)]
+            parts = [(nc.gpsimd, 0, T)] if b < KB - 1 else [(nc.gpsimd, 0, T // 2), (nc.gpsimd, T // 2, 768), (nc.vector, 768, T)]
             for eng, c0, c1 in parts:
                 for r, lp in enumerate((lp1, lp2)):
                     nc.vector.tensor_copy(y[r][:, c0:c1], dx[b][:].indirect(lp[:, c0 // 16:c1 // 16]))

@@ -97,12 +97,13 @@ def tile_moe_bdx_glu_relu_kernel(tc, dyT, a1, a3, w2_words, w2_scales, w1_words,
 
         nc.sync.dma_start(lo[:], offs)
         load_win(0, 0)
-        load_gate(0)
-        load_win(0, 1)
+        nc.sync.dma_start(gt[:, 0:256], gate[0:P, 0:256])
+        nc.sync.dma_start(gt[:, 256:C], gate[0:P, 256:C])
+        load_w2(0)
         load_gate(1)
+        load_win(0, 1)
         load_win(0, 2)
         load_win(0, 3)
-        load_w2(0)
         for t in range(PACK):
             load_win(1, t)
         load_w2(1)
@@ -203,7 +204,7 @@ def tile_moe_bdx_glu_relu_kernel(tc, dyT, a1, a3, w2_words, w2_scales, w1_words,
                         rhs=dq[e, x][:].bitcast(E5X4), rhs_scale=ds[e, x][:], start=(x == 1), stop=(x == 0))
                 nc.scalar.copy(out=dx[b][:, e * C:(e + 1) * C], in_=acc[:])
 
-        gathers(0, 0, (512, 512))
+        gathers(0, 0, (256, 256, 512))
         permute(0)
         quant_g(0, 0)
         permute(1)

from contextlib import ExitStack

import concourse.mybir as mybir

K, T, E, C, H, N = 384, 1024, 4, 512, 512, 1024
S = E * C
P = 128
PACK = 4
PASSES = N // (P * PACK)
KB = K // P

FLOPS = 2 * S * (N * H + 2 * H * K)
W = T + 16
BYTES = 4 * (N * T + 2 * H * S + S + K * T) + E * (N * H + 2 * H * K) // 2 + E * (N * H + 2 * H * K) // 32 + 2 * (S + 2 * T)

F32 = mybir.dt.float32
BF16 = mybir.dt.bfloat16
I32 = mybir.dt.int32
U32 = mybir.dt.uint32
U16 = mybir.dt.uint16
U8 = mybir.dt.uint8
E5X4 = mybir.dt.float8_e5m2_x4
E2X4 = mybir.dt.float4_e2m1fn_x4
MULT = mybir.AluOpType.mult
ADD = mybir.AluOpType.add
RELU = mybir.ActivationFunctionType.Relu
SIGN = mybir.ActivationFunctionType.Sign


def tile_moe_bdx_glu_relu_kernel(tc, dyT, a1, a3, w2_words, w2_scales, w1_words, w1_scales, w3_words, w3_scales, gate, offs, pos1, pos2, out):
    nc = tc.nc
    with ExitStack() as ctx:
        keep = ctx.enter_context(tc.tile_pool(name="keep", bufs=1))
        wins = ctx.enter_context(tc.tile_pool(name="wins", bufs=8))
        two = ctx.enter_context(tc.tile_pool(name="two", bufs=2))
        four = ctx.enter_context(tc.tile_pool(name="four", bufs=4))
        pdh = ctx.enter_context(tc.psum_pool(name="pdh", bufs=5))
        pdx = ctx.enter_context(tc.psum_pool(name="pdx", bufs=3))

        lo = keep.tile([P, S // 16], U16, name="lo")
        lp1 = keep.tile([P, T // 16], U16, name="lp1")
        lp2 = keep.tile([P, T // 16], U16, name="lp2")
        gt = keep.tile([P, S], F32, name="gt")
        w2p = keep.tile([P, E * PASSES * 2 * H], U8, name="w2p", align_bytes=64)
        w2r = keep.tile([P, PASSES * H], U8, name="w2r", align_bytes=64)
        w2s = keep.tile([P, E * PASSES * H], U8, name="w2s", align_bytes=64)
        wk = [keep.tile([P, E * 2 * K], U8, name=f"wk{x}", align_bytes=64) for x in range(2)]
        wks = [keep.tile([P, E * K], U8, name=f"wks{x}", align_bytes=64) for x in range(2)]
        dx = [keep.tile([P, S], F32, name=f"dx{b}") for b in range(KB)]
        for t in [w2r, w2s] + wks:
            nc.gpsimd.memset(t[:].bitcast(I32), 0)

        dy_v = dyT.rearrange("(s p t) c -> s t p c", s=PASSES, t=PACK)
        win = {}

        def load_win(s, t):
            win[s, t] = wins.tile([P, W], F32, name="win")
            nc.gpsimd.memset(win[s, t][:, T:], 0.0)
            nc.sync.dma_start(win[s, t][:, 0:T], dy_v[s, t])

        def load_gate(e):
            nc.sync.dma_start(gt[:, e * C:(e + 1) * C], gate[0:P, e * C:(e + 1) * C])

        def load_scales(tile, dram, n):
            v = dram.bitcast(I32).rearrange("e s (q r) i -> r q (e s) i", r=4)
            for r in range(4):
                nc.sync.dma_start(tile[r:P:32, :].bitcast(I32).rearrange("q (g i) -> q g i", i=n // 4), v[r])

        def load_w2_scales():
            for e in range(E):
                nc.sync.dma_start(w2r[32 * e:32 * e + 16, :].bitcast(I32).rearrange("f (s i) -> f s i", s=PASSES), w2_scales[e].bitcast(I32).rearrange("s f i -> f s i"))

        def spread_w2_scales():
            n = PASSES * H
            w2q = keep.tile([P, n], U8, name="w2q", align_bytes=64)
            nc.vector.tensor_copy(out=w2q[:].rearrange("p (s t m) -> p s t m", s=PASSES, t=PACK), in_=w2r[:].rearrange("p (s m t) -> p s t m", s=PASSES, t=PACK))
            for e in range(E):
                for r in range(4):
                    nc.sync.dma_start(w2s[r:P:32, e * n:(e + 1) * n].bitcast(I32), w2q[32 * e + r:32 * e + 16:4, :].bitcast(I32))

        w2raw = {}

        def load_w2(e):
            w2raw[e] = two.tile([P, PASSES * 2 * H], U8, name="w2raw")
            nc.sync.dma_start(w2raw[e][:].bitcast(I32).rearrange("p (s b) -> p s b", s=PASSES), w2_words[e].bitcast(I32).rearrange("s p b -> p s b"))

        def load_wk(x, dram):
            nc.sync.dma_start(wk[x][:].bitcast(I32).rearrange("p (e b) -> p e b", e=E), dram.bitcast(I32).rearrange("e s p b -> p (e s) b"))

        am = {}
        a_v = [a.rearrange("(p t) (e c) -> e p t c", t=PACK, e=E) for a in (a3, a1)]

        def load_a(e):
            am[e] = two.tile([P, 2, PACK, C], F32, name="am")
            for x in (1, 0):
                nc.sync.dma_start(am[e][:, x], a_v[x][e])

        nc.sync.dma_start(lo[:], offs)
        load_win(0, 0)
        nc.sync.dma_start(gt[:, 0:256], gate[0:P, 0:256])
        nc.sync.dma_start(gt[:, 256:C], gate[0:P, 256:C])
        load_w2(0)
        load_gate(1)
        load_win(0, 1)
        load_win(0, 2)
        load_win(0, 3)
        for t in range(PACK):
            load_win(1, t)
        load_w2(1)
        load_w2_scales()
        load_a(0)
        load_gate(2)
        load_gate(3)
        load_w2(2)
        load_wk(0, w1_words)
        load_wk(1, w3_words)
        load_scales(wks[0], w1_scales, K)
        load_scales(wks[1], w3_scales, K)
        load_w2(3)
        load_a(1)
        load_a(2)
        load_a(3)
        nc.sync.dma_start(lp1[:], pos1)
        nc.sync.dma_start(lp2[:], pos2)

        def permute(e):
            n = PASSES * 2 * H
            nc.vector.tensor_copy(
                out=w2p[:, e * n:(e + 1) * n].bitcast(U16).rearrange("p (s t m) -> p s t m", s=PASSES, t=PACK),
                in_=w2raw[e][:].bitcast(U16).rearrange("p (s m t) -> p s t m", s=PASSES, t=PACK))

        gi, gq, gs = {}, {}, {}

        def gathers(e0, s, cuts=(1024,)):
            g4 = two.tile([P, PACK, 2 * C], F32, name="g4")
            for t in range(PACK):
                j = 0
                for n in (cuts if t == 0 else (1024,)):
                    j0 = e0 * C + j
                    nc.vector.tensor_tensor(g4[:, t, j:j + n], win[s, t][:].indirect(lo[:, j0 // 16:(j0 + n) // 16]), gt[:, j0:j0 + n], MULT)
                    j += n
            for e in (e0, e0 + 1):
                gi[e, s] = two.tile([P, C * PACK], BF16, name="gi", align_bytes=64)
                nc.scalar.copy(out=gi[e, s][:].rearrange("p (c i t) -> p c t i", i=4, t=PACK), in_=g4[:, :, (e - e0) * C:(e - e0 + 1) * C].rearrange("p t (c i) -> p c t i", i=4))

        def quant_g(e, s):
            gq[e, s] = four.tile([P, C], U32, name="gq", align_bytes=64)
            gs[e, s] = four.tile([P, C], U8, name="gs", align_bytes=64)
            nc.vector.quantize_mx(out=gq[e, s][:].bitcast(E5X4), scales=gs[e, s][:], in_=gi[e, s][:])

        hs = {}

        def mm_dh(e):
            hs[e] = two.tile([P, PACK, C], F32, name="hs")
            for t in range(PACK):
                dh = pdh.tile([P, C], F32, name="dh")
                for s in range(PASSES):
                    b = ((e * PASSES + s) * PACK + t) * P
                    nc.tensor.matmul_mx(
                        out=dh[:], lhsT=w2p[:, 2 * b:2 * (b + P)].bitcast(E2X4), lhsT_scale=w2s[:, b:b + P],
                        rhs=gq[e, s][:].bitcast(E5X4), rhs_scale=gs[e, s][:], start=(s == 0), stop=(s == PASSES - 1))
                nc.scalar.copy(out=hs[e][:, t, :], in_=dh[:])

        mk = {}

        def masks(e):
            mk[e] = two.tile([P, C * PACK], BF16, name="mk")
            nc.scalar.activation(am[e][:, 1], am[e][:, 1], RELU)
            nc.scalar.activation(mk[e][:].rearrange("p (c i t) -> p c t i", i=4, t=PACK), am[e][:, 1].rearrange("p t (c i) -> p c t i", i=4), SIGN)

        zi = {}

        def quads(ap):
            return ap.rearrange("p t (c i) -> p c t i", i=4)

        def woven(ap):
            return ap.rearrange("p (c i t) -> p c t i", i=4, t=PACK)

        def product(e, x, parts=1):
            if e not in zi:
                zi[e] = two.tile([P, 2, C * PACK], BF16, name="zi", align_bytes=64)
            w = P // parts
            for c in range(0, P, w):
                nc.vector.tensor_tensor(woven(zi[e][:, x])[:, c:c + w], quads(hs[e][:])[:, c:c + w], quads(am[e][:, x])[:, c:c + w], MULT)

        dq, ds = {}, {}

        def mask_d(e):
            nc.vector.tensor_tensor(zi[e][:, 0], zi[e][:, 0], mk[e][:], MULT)

        def quant_d(e):
            for x in (1, 0):
                dq[e, x] = two.tile([P, C], U32, name=f"dq{x}", align_bytes=64)
                ds[e, x] = two.tile([P, C], U8, name=f"ds{x}", align_bytes=64)
                nc.vector.quantize_mx(out=dq[e, x][:].bitcast(E5X4), scales=ds[e, x][:], in_=zi[e][:, x])

        def mm_dx(e):
            for b in range(KB):
                acc = pdx.tile([P, C], F32, name="acc")
                for x in (1, 0):
                    c = e * K + b * P
                    nc.tensor.matmul_mx(
                        out=acc[:], lhsT=wk[x][:, 2 * c:2 * (c + P)].bitcast(E2X4), lhsT_scale=wks[x][:, c:c + P],
                        rhs=dq[e, x][:].bitcast(E5X4), rhs_scale=ds[e, x][:], start=(x == 1), stop=(x == 0))
                nc.scalar.copy(out=dx[b][:, e * C:(e + 1) * C], in_=acc[:])

        gathers(0, 0, (256, 256, 512))
        permute(0)
        quant_g(0, 0)
        permute(1)
        gathers(0, 1)
        quant_g(1, 0)
        spread_w2_scales()
        quant_g(0, 1)
        mm_dh(0)
        quant_g(1, 1)
        permute(2)
        gathers(2, 0)
        masks(0)
        mm_dh(1)
        product(0, 0)
        product(0, 1)
        mask_d(0)
        permute(3)
        quant_d(0)
        quant_g(2, 0)
        quant_g(3, 0)
        gathers(2, 1)
        mm_dx(0)
        masks(1)
        product(1, 0)
        quant_g(2, 1)
        mm_dh(2)
        product(1, 1, 2)
        quant_g(3, 1)
        mm_dh(3)
        mask_d(1)
        quant_d(1)
        mm_dx(1)
        masks(2)
        product(2, 0)
        product(2, 1)
        masks(3)
        mask_d(2)
        quant_d(2)
        mm_dx(2)
        product(3, 0)
        product(3, 1)
        mask_d(3)
        quant_d(3)
        mm_dx(3)

        for b in range(KB):
            y = [wins.tile([P, W], F32, name="win") for r in range(2)]
            parts = [(nc.gpsimd, 0, T)] if b < KB - 1 else [(nc.gpsimd, 0, T // 2), (nc.gpsimd, T // 2, 768), (nc.vector, 768, T)]
            for eng, c0, c1 in parts:
                for r, lp in enumerate((lp1, lp2)):
                    nc.vector.tensor_copy(y[r][:, c0:c1], dx[b][:].indirect(lp[:, c0 // 16:c1 // 16]))
                eng.tensor_tensor(y[0][:, c0:c1], y[0][:, c0:c1], y[1][:, c0:c1], ADD)
                nc.sync.dma_start(out[b * P:(b + 1) * P, c0:c1], y[0][:, c0:c1])
